import numpy as np
import ml_dtypes


def mxq(x, axis, fmt="e4m3"):
    dtype, down = {"e4m3": (ml_dtypes.float8_e4m3fn, 7), "e5m2": (ml_dtypes.float8_e5m2, 14)}[fmt]
    v = np.moveaxis(np.asarray(x, np.float32).astype(ml_dtypes.bfloat16).astype(np.float64), axis, -1)
    blocks = v.reshape(v.shape[:-1] + (-1, 32))
    amax = np.abs(blocks).max(-1, keepdims=True)
    byte = np.maximum(np.where(amax > 0, np.frexp(amax)[1] - 1 + 127, 0) - down, 1)
    scale = np.exp2(byte - 127.0)
    codes = (blocks / scale).astype(np.float32).astype(dtype).astype(np.float64)
    return np.moveaxis((codes * scale).reshape(v.shape), -1, axis)


WIDE = False


def mx_kscale(k):
    if not WIDE:
        return np.ones(k)
    levels = np.array([10, -10, 5, -5, 0])
    if k % 512:
        return np.exp2(np.random.permutation(np.resize(levels, k // 32))).repeat(32)
    a = np.empty((k // 512, 16))
    for p in range(k // 512):
        a[p, :8] = np.random.permutation(np.resize(levels, 8))
        for g in range(8):
            far = levels[np.abs(levels - a[p, g]) >= 10]
            a[p, g + 8] = far[np.random.randint(len(far))]
    return np.exp2(a.ravel()).repeat(32)


BF16 = ml_dtypes.bfloat16


def bf(x):
    return np.asarray(x, np.float32).astype(BF16)


def f64(x):
    return np.asarray(x).astype(np.float64)


E2M1 = np.array([0.0, 0.5, 1.0, 1.5, 2.0, 3.0, 4.0, 6.0, -0.0, -0.5, -1.0, -1.5, -2.0, -3.0, -4.0, -6.0])


def pack_weight(w, fmt):
    k, n = w.shape
    w = f64(bf(w)).reshape(k // 32, 32, n)
    amax = np.abs(w).max(1)
    if fmt == "e4m3":
        byte = np.frexp(amax)[1] - 1 + 127 - 7
    else:
        mant, ex = np.frexp(amax / 6.0)
        byte = np.where(mant > 0.5, ex, ex - 1) + 127
    byte = np.clip(np.where(amax > 0, byte, 1), 1, 254)
    scaled = (w * np.exp2(127.0 - byte)[:, None, :]).reshape(k, n).astype(np.float32)
    by_word = np.ascontiguousarray(scaled.reshape(k // 512, 128, 4, n).transpose(0, 1, 3, 2))
    if fmt == "e4m3":
        words = by_word.astype(ml_dtypes.float8_e4m3fn).view(np.uint8)
    else:
        c = by_word.astype(ml_dtypes.float4_e2m1fn).view(np.uint8) & 0xF
        words = c[..., 0::2] | (c[..., 1::2] << 4)
    return np.ascontiguousarray(words), np.ascontiguousarray(byte.astype(np.uint8).reshape(k // 512, 16, n))


def unpack_weight(words, scales, fmt):
    g, p, n, _ = words.shape
    if fmt == "e4m3":
        vals = np.ascontiguousarray(words).view(ml_dtypes.float8_e4m3fn).astype(np.float64)
    else:
        nib = np.empty((g, p, n, 4), np.uint8)
        nib[..., 0::2] = words & 0xF
        nib[..., 1::2] = words >> 4
        vals = E2M1[nib]
    vals = vals * np.repeat(np.exp2(scales.astype(np.float64) - 127.0), 8, axis=1)[..., None]
    return vals.transpose(0, 1, 3, 2).reshape(g * 512, n)
def pack4(w):
    words, scales = pack_weight(w, "e2m1")
    return words.reshape(words.shape[0], 128, -1), scales


def unpack4(words, scales):
    return unpack_weight(words.reshape(words.shape[0], 128, -1, 2), scales, "e2m1")


M, D, F = 1024, 1024, 1536


def sigmoid(x):
    return 1.0 / (1.0 + np.exp(-x))


def setup_inputs():
    s, t, v = mx_kscale(D), mx_kscale(F), mx_kscale(F)
    dout = bf(np.random.standard_normal((M, D)))
    ls = bf((1.0 + 0.1 * np.random.standard_normal(D)) * s)
    gate = bf(1.5 * np.random.standard_normal((M, F)))
    up = bf(np.random.standard_normal((M, F)) * v)
    gain = bf(1.0 + 0.1 * np.random.standard_normal(D))
    a_words, a_scales = pack4(np.random.standard_normal((D, F)) / np.sqrt(D) / s[:, None] * t)
    b_words, b_scales = pack_weight(np.random.standard_normal((F, D)) / np.sqrt(F) / t[:, None] / v[:, None], "e4m3")
    c_words, c_scales = pack_weight(np.random.standard_normal((F, D)) / np.sqrt(F) / t[:, None], "e4m3")
    return {"dout": dout, "ls": ls, "gate": gate, "up": up, "gain": gain,
            "a_words": a_words, "a_scales": a_scales,
            "b_words": b_words, "b_scales": b_scales,
            "c_words": c_words, "c_scales": c_scales}


def reference(dout, ls, gate, up, gain, a_words, a_scales, b_words, b_scales, c_words, c_scales):
    d = f64(dout)
    dy = d * f64(ls)
    dh = mxq(dy, 1, "e4m3") @ unpack4(a_words, a_scales)
    z = f64(gate)
    sg = sigmoid(z)
    dup = dh * (z * sg)
    dgate = dh * f64(up) * (sg * (1.0 + z * (1.0 - sg)))
    via_gate = mxq(dgate, 1, "e4m3") @ unpack_weight(b_words, b_scales, "e4m3")
    via_up = mxq(dup, 1, "e4m3") @ unpack_weight(c_words, c_scales, "e4m3")
    return d + f64(gain) * (via_gate + via_up)

from contextlib import ExitStack

import concourse.mybir as mybir
from concourse.masks import make_identity

M, D, F = 1024, 1024, 1536
FLOPS = 3 * 2 * M * D * F

F32 = mybir.dt.float32
BF16 = mybir.dt.bfloat16
I32 = mybir.dt.int32
U32 = mybir.dt.uint32
U8 = mybir.dt.uint8
FP8X4 = mybir.dt.float8_e4m3fn_x4
FP4X4 = mybir.dt.float4_e2m1fn_x4
ALU = mybir.AluOpType
ACT = mybir.ActivationFunctionType

P = 128
TILES = M // P
W = 512
CH = F // W
KD = D // W
G_CHUNKS = (2,)


def tile_swiglu_block_backward_f7_kernel(
    tc, dout, ls, gate, up, gain, a_words, a_scales, b_words, b_scales, c_words, c_scales, out
):
    nc = tc.nc
    with ExitStack() as ctx:
        keep = ctx.enter_context(tc.tile_pool(name="keep", bufs=1))
        work = ctx.enter_context(tc.tile_pool(name="work", bufs=2))
        psum = ctx.enter_context(tc.psum_pool(name="psum", bufs=3))
        ctx.enter_context(tc.manual_schedule())

        dout_sb = [keep.tile([P, D], BF16, name=f"dout{i}", align_bytes=64) for i in range(TILES)]
        gate_sb = [keep.tile([P, F], BF16, name=f"gate{i}", align_bytes=64) for i in range(TILES)]
        up_sb = [keep.tile([P, F], BF16, name=f"up{i}", align_bytes=64) for i in range(TILES)]
        a_sb = [keep.tile([P, 2 * F], U8, name=f"a{g}", align_bytes=64) for g in range(KD)]
        a_pl = keep.tile([P, KD, F], U8, name="a_pl", align_bytes=64)
        b_sb = [keep.tile([P, D], U32, name=f"b{g}", align_bytes=64) for g in range(CH)]
        c_sb = [keep.tile([P, D], U32, name=f"c{g}", align_bytes=64) for g in range(CH)]
        b_pl = keep.tile([P, CH, D], U8, name="b_pl", align_bytes=64)
        c_pl = keep.tile([P, CH, D], U8, name="c_pl", align_bytes=64)
        ident = keep.tile([P, P], F32, name="ident")
        ones = keep.tile([P, P], BF16, name="ones")
        rows = keep.tile([P, 2 * D], BF16, name="rows", align_bytes=64)
        ls_sb = keep.tile([P, D], BF16, name="ls_sb", align_bytes=64)
        gain_sb = keep.tile([P, D], BF16, name="gain_sb", align_bytes=64)
        dummy = keep.tile([P, 1], F32, name="dummy")

        nc.vector.memset(dummy[:], 0.0)
        nc.scalar.activation(out=dummy[:], in_=dummy[:], func=ACT.Silu)
        nc.vector.memset(rows[:].bitcast(U32), 0)
        nc.vector.memset(a_pl[:].rearrange("p g n -> p (g n)").bitcast(U32), 0)
        nc.vector.memset(ones[:], 1.0)
        make_identity(nc, ident[:])
        nc.vector.memset(b_pl[:].rearrange("p g n -> p (g n)").bitcast(U32), 0)
        nc.vector.memset(c_pl[:].rearrange("p g n -> p (g n)").bitcast(U32), 0)

        def load_scales(plane, scales):
            for q in range(4):
                nc.sync.dma_start(
                    out=plane[32 * q : 32 * q + 4, :, :].bitcast(I32),
                    in_=scales[:, 4 * q : 4 * q + 4, :].rearrange("g r n -> r g n").bitcast(I32),
                )

        def load(tiles, src, i):
            nc.sync.dma_start(out=tiles[i][:], in_=src[i * P : (i + 1) * P, :])

        def load_fp8(tiles, words, g):
            nc.sync.dma_start(out=tiles[g][:].bitcast(I32), in_=words[g].rearrange("p n t -> p (n t)").bitcast(I32))

        load(dout_sb, dout, 0)
        nc.sync.dma_start(out=rows[0:1, 0:D], in_=ls.unsqueeze(0))
        load(gate_sb, gate, 0)
        load(up_sb, up, 0)
        nc.sync.dma_start(out=rows[0:1, D : 2 * D], in_=gain.unsqueeze(0))
        load_scales(a_pl, a_scales)
        for g in range(KD):
            nc.sync.dma_start(out=a_sb[g][:].bitcast(I32), in_=a_words[g].bitcast(I32))
        load(dout_sb, dout, 1)
        load(gate_sb, gate, 1)
        load(up_sb, up, 1)
        load(dout_sb, dout, 2)
        load_scales(c_pl, c_scales)
        load_scales(b_pl, b_scales)
        load_fp8(c_sb, c_words, 0)
        load_fp8(b_sb, b_words, 0)
        load(gate_sb, gate, 2)
        load_fp8(c_sb, c_words, 1)
        load_fp8(b_sb, b_words, 1)
        load(up_sb, up, 2)
        load_fp8(c_sb, c_words, 2)
        load_fp8(b_sb, b_words, 2)
        for i in range(3, TILES):
            load(dout_sb, dout, i)
            load(gate_sb, gate, i)
            load(up_sb, up, i)

        def spread(dst, c0):
            for h in range(D // W):
                bank = psum.tile([P, W], F32, tag="acc", bufs=3, name="bank")
                nc.tensor.matmul(bank[:], lhsT=ones[:], rhs=rows[:, c0 + h * W : c0 + (h + 1) * W], start=True, stop=True)
                nc.scalar.copy(out=dst[:, h * W : (h + 1) * W], in_=bank[:])

        live = {}

        def ls_mul(i):
            t = work.tile([P, D], BF16, tag="dyn", bufs=2, align_bytes=64, name="dyn")
            nc.vector.tensor_tensor(out=t[:], in0=dout_sb[i][:], in1=ls_sb[:], op=ALU.mult)
            live["dyn", i] = t

        def turn_dy(i):
            words = live["dyn", i][:].bitcast(F32)
            xt = psum.tile([P, 4, P], F32, tag="xt", bufs=2, name="xt")
            for g in range(KD):
                for u in range(2):
                    nc.tensor.transpose(xt[:, 2 * g + u, :], words[:, 256 * g + u : 256 * (g + 1) : 2], ident[:])
            grp = work.tile([P, KD * P * 4], BF16, tag="dyg", bufs=2, align_bytes=64, name="dyg")
            live["xdy", i] = xt
            live["dyg", i] = grp

        def group_dy(i):
            nc.scalar.copy(
                out=live["dyg", i][:].bitcast(F32).rearrange("p (g m u) -> p g m u", g=KD, u=2),
                in_=live["xdy", i][:].rearrange("p (g u) m -> p g m u", g=KD),
            )

        def quant_dy(i):
            codes = work.tile([P, KD * P], U32, tag="dyc", bufs=2, align_bytes=64, name="dyc")
            plane = work.tile([P, KD * P], U8, tag="dys", bufs=2, align_bytes=64, name="dys")
            nc.vector.quantize_mx(out=codes[:].bitcast(FP8X4), scales=plane[:], in_=live["dyg", i][:])
            live["dyc", i] = (codes, plane)

        def stage1(i, c):
            codes, plane = live["dyc", i]
            dh = psum.tile([P, W], F32, tag="dh", bufs=3, name="dh")
            for g in range(KD):
                nc.tensor.matmul_mx(
                    out=dh[:],
                    lhsT=codes[:, g * P : (g + 1) * P].bitcast(FP8X4),
                    lhsT_scale=plane[:, g * P : (g + 1) * P],
                    rhs=a_sb[g][:, 2 * c * W : 2 * (c + 1) * W].bitcast(FP4X4),
                    rhs_scale=a_pl[:, g, c * W : (c + 1) * W],
                    start=(g == 0),
                    stop=(g == KD - 1),
                )
            live["dh", i, c] = dh

        def new_factor(kind, i, c):
            t = work.tile([P, W], F32, tag=kind, bufs=6, align_bytes=64, name=kind)
            live[kind, i, c] = t
            return t

        def act_tn(i, c):
            z = gate_sb[i][:, c * W : (c + 1) * W]
            nc.scalar.activation(out=new_factor("n", i, c)[:], in_=z, func=ACT.Silu, scale=-1.0)
            nc.scalar.activation(out=new_factor("th", i, c)[:], in_=z, func=ACT.Tanh, scale=-0.5)
            if c in G_CHUNKS:
                nc.scalar.activation(out=new_factor("t1", i, c)[:], in_=live["th", i, c][:], func=ACT.Identity, bias=-1.0)

        def act_h(i, c):
            nc.scalar.activation(out=new_factor("h", i, c)[:], in_=gate_sb[i][:, c * W : (c + 1) * W], func=ACT.Silu)

        def fac_a(i, c):
            nc.vector.scalar_tensor_tensor(
                out=new_factor("a", i, c)[:], in0=live["n", i, c][:], scalar=1.0, in1=up_sb[i][:, c * W : (c + 1) * W],
                op0=ALU.subtract, op1=ALU.mult,
            )

        def fac_k(i, c):
            k = new_factor("k", i, c)
            if c in G_CHUNKS:
                nc.gpsimd.tensor_tensor(out=k[:], in0=live["t1", i, c][:], in1=live["a", i, c][:], op=ALU.mult)
            else:
                nc.vector.scalar_tensor_tensor(
                    out=k[:], in0=live["th", i, c][:], scalar=1.0, in1=live["a", i, c][:],
                    op0=ALU.subtract, op1=ALU.mult,
                )

        def dup_dgate(i, c):
            dh = live["dh", i, c]
            dd = work.tile([P, 2, W], BF16, tag="dd", bufs=3, align_bytes=64, name="dd")
            nc.vector.tensor_tensor(out=dd[:, 0, :], in0=dh[:], in1=live["h", i, c][:], op=ALU.mult)
            nc.vector.scalar_tensor_tensor(
                out=dd[:, 1, :], in0=dh[:], scalar=0.5, in1=live["k", i, c][:], op0=ALU.mult, op1=ALU.mult
            )
            live["dd", i, c] = dd

        def turn_d(i, c):
            xt = psum.tile([P, 4, P], F32, tag="xt", bufs=2, name="xt")
            for s in range(2):
                words = live["dd", i, c][:, s, :].bitcast(F32)
                for u in range(2):
                    nc.tensor.transpose(xt[:, 2 * s + u, :], words[:, u : W // 2 : 2], ident[:])
            live["xd", i, c] = xt

        def group_d(i, c):
            grp = work.tile([P, 2 * W], BF16, tag="ddg", bufs=3, align_bytes=64, name="ddg")
            nc.scalar.copy(
                out=grp[:].bitcast(F32).rearrange("p (s m u) -> p s m u", s=2, u=2),
                in_=live["xd", i, c][:].rearrange("p (s u) m -> p s m u", s=2),
            )
            live["ddg", i, c] = grp

        def quant_d(i, c):
            codes = work.tile([P, 2 * P], U32, tag="ddc", bufs=6, align_bytes=64, name="ddc")
            plane = work.tile([P, 2 * P], U8, tag="dds", bufs=6, align_bytes=64, name="dds")
            nc.vector.quantize_mx(out=codes[:].bitcast(FP8X4), scales=plane[:], in_=live["ddg", i, c][:])
            live["ddc", i, c] = (codes, plane)

        def stage2(i, c):
            codes, plane = live["ddc", i, c]
            for h in range(D // W):
                if c == 0:
                    live["acc", i, h] = psum.tile([P, W], F32, tag="acc", bufs=3, name="acc")
                cols = slice(h * W, (h + 1) * W)
                for s, (w_sb, w_pl) in enumerate(((c_sb, c_pl), (b_sb, b_pl))):
                    nc.tensor.matmul_mx(
                        out=live["acc", i, h][:],
                        lhsT=codes[:, s * P : (s + 1) * P].bitcast(FP8X4),
                        lhsT_scale=plane[:, s * P : (s + 1) * P],
                        rhs=w_sb[c][:, cols].bitcast(FP8X4),
                        rhs_scale=w_pl[:, c, cols],
                        start=(c == 0 and s == 0),
                        stop=(c == CH - 1 and s == 1),
                    )

        def scale(i, h):
            cols = slice(h * W, (h + 1) * W)
            res = work.tile([P, W], F32, tag="res", bufs=4, align_bytes=64, name="res")
            nc.vector.tensor_tensor(out=res[:], in0=live["acc", i, h][:], in1=gain_sb[:, cols], op=ALU.mult)
            live["res", i, h] = res

        def finish(i, h, engine):
            cols = slice(h * W, (h + 1) * W)
            res = live["res", i, h]
            dz = work.tile([P, W], F32, tag="dz", bufs=4, align_bytes=64, name="dz")
            engine.tensor_tensor(out=dz[:], in0=res[:], in1=dout_sb[i][:, cols], op=ALU.add)
            nc.sync.dma_start(out=out[i * P : (i + 1) * P, cols], in_=dz[:])

        N = TILES * CH

        def at(f, j):
            if 0 <= j < N:
                f(j // CH, j % CH)

        spread(ls_sb, 0)
        ls_mul(0)
        turn_dy(0)
        act_tn(0, 0)
        group_dy(0)
        fac_a(0, 0)
        quant_dy(0)
        fac_k(0, 0)
        for c in range(CH):
            stage1(0, c)
        act_tn(0, 1)
        fac_a(0, 1)
        ls_mul(1)
        turn_dy(1)
        fac_k(0, 1)
        act_h(0, 0)
        act_tn(0, 2)
        group_dy(1)
        fac_a(0, 2)
        quant_dy(1)
        fac_k(0, 2)
        spread(gain_sb, D)
        act_tn(1, 0)

        for j in range(N + 1):
            i, c = j // CH, j % CH
            at(act_h, j + 1)
            at(act_tn, j + 4)
            if i > 0 and c > 0:
                scale(i - 1, c - 1)
                finish(i - 1, c - 1, nc.gpsimd)
            at(dup_dgate, j)
            if c not in G_CHUNKS:
                at(fac_a, j + 3)
            at(turn_d, j)
            if c == 0 and i + 2 < TILES:
                ls_mul(i + 2)
            if c == 1 and i + 2 < TILES:
                turn_dy(i + 2)
            at(quant_d, j - 1)
            at(group_d, j)
            if c == 1 and i + 2 < TILES:
                group_dy(i + 2)
            if c == 2 and i + 2 < TILES:
                quant_dy(i + 2)
            if c in G_CHUNKS:
                at(fac_a, j + 3)
            at(fac_k, j + 3)
            at(stage1, j + 3)
            at(stage2, j - 1)
        for h in range(D // W):
            scale(TILES - 1, h)
        for h in range(D // W):
            finish(TILES - 1, h, nc.vector)
